import numpy as np, ml_dtypes
CORES = [36,164,52,180,100,228,116,244]
N = 8
BF = ml_dtypes.bfloat16
def entries(a):
    return np.ascontiguousarray(a.T).reshape(-1)
def table(e):
    return np.ascontiguousarray(np.reshape(e, (-1, 16)).T).astype(np.int32)
def f(rng, *shape):
    return (rng.standard_normal(shape, dtype=np.float32) * np.exp2(rng.integers(-2, 3, shape[:-1] + (1,)))).astype(BF)
def wide(rng, *shape):
    v = f(rng, *shape).astype(np.float32); k = shape[:-2] + (1, shape[-1])
    return (v * np.exp2(rng.integers(-6, 7, k)) * (rng.random(k) > 0.0625)).astype(BF)
R, S1, S2, CAPP = 2048, 256, 1024, 16
T1, T2 = 0, 100
def orders(rng):
    return np.stack([rng.permutation(R) for r in range(N)])
def values(rng, order, n1, m, lo):
    v = rng.integers(-60, 1, (N, R))
    for r in range(N):
        v[r, order[r, :n1[r]]] = rng.integers(1, 5, n1[r]); v[r, order[r, :m[r]]] = rng.integers(lo[r], 256, m[r])
    x = f(rng, N, 16, R); x[:, 0] = v.astype(np.float32).astype(BF); return x
def some(rng, order, n1, m, *shape):
    top = np.array([m, n1, R])[rng.integers(0, 3, shape)]
    return order[(rng.random(shape) * top).astype(np.int64)]
def ghosts(rng, r, *shape):
    return R + ((r + 1 + rng.integers(0, N - 1, shape)) % N) * CAPP + rng.integers(0, CAPP, shape)
def draw(rng, order, n1, m, lo):
    x = values(rng, order, n1, m, lo); nb = []; bd = []
    for r in range(N):
        nb.append(np.where(rng.random((6, R)) < 0.7, some(rng, order[r], n1[r], m[r], 6, R), ghosts(rng, r, 6, R)))
        bd.append(table(some(rng, order[r], n1[r], m[r], N * CAPP)))
    return {"x": x, "nb": np.stack(nb).astype(np.int32), "bd": np.stack(bd)}
def setup_inputs(rng):
    return draw(rng, orders(rng), rng.integers(3 * S1 // 4, S1 + 1, N), np.full(N, S2 // 8), np.full(N, 40))
def setup_inputs_full(rng):
    order = orders(rng); a = int(rng.integers(0, N)); order[a] = np.arange(R); order[(a + 1) % N] = np.arange(R)[::-1]
    return draw(rng, order, np.full(N, S1), np.full(N, S2 // 8), np.full(N, 200))
def setup_inputs_ties(rng):
    order = orders(rng); n1 = rng.integers(3 * S1 // 4, S1 + 1, N); m = S2 // 8
    d = draw(rng, order, n1, np.full(N, m), np.full(N, 40)); x, nb = d["x"], d["nb"]; bd = []
    for r in range(N):
        h = order[r, :m]; c = order[r, n1[r]:]
        x[r, 0, h] = rng.integers(99, 102, m).astype(np.float32).astype(BF); x[r, 0, c] = rng.integers(-1, 1, len(c)).astype(np.float32).astype(BF)
        nb[r][:, h] = np.where(rng.random((6, m)) < 0.5, h[rng.integers(0, m, (6, m))], ghosts(rng, r, 6, m))
        nb[r][:, h[0]] = h[0]; x[r, 0, h[0]] = 100; nb[r][:, h[1]] = h[1]; x[r, 0, h[1]] = 101
        bd.append(table(h[rng.integers(0, m, N * CAPP)]))
    d["bd"] = np.stack(bd); return d
def setup_inputs_thin(rng):
    order = orders(rng); n1 = rng.integers(3 * S1 // 4, S1 + 1, N); m = np.minimum(S2 // 4, n1)
    d = draw(rng, order, n1, m, np.full(N, 40)); x, nb, bd = d["x"], d["nb"], d["bd"]; first = int(rng.integers(0, 6))
    for r in range(N):
        k = int(m[r]); h = order[r, :k]; c = order[r, n1[r]:]
        x[r, 0, h] = rng.integers(101, 104, k).astype(np.float32).astype(BF)
        nb[r][:, h] = np.where(rng.random((6, k)) < 0.5, h[rng.integers(0, k, (6, k))], ghosts(rng, r, 6, k))
        nb[r][(first + r) % 6, h] = c[rng.integers(0, len(c), k)]
        bd[r] = table(h[rng.integers(0, k, N * CAPP)])
    return d
def setup_inputs_far(rng):
    order = orders(rng); n1 = rng.integers(3 * S1 // 4, S1 + 1, N); m = np.full(N, S2 // 8); lo = np.full(N, 40); a = int(rng.integers(0, N)); b = (a + 1) % N; s = int(rng.integers(1, N))
    n1[a] = S1 // 8; m[a] = S2 // 64; lo[a] = 200
    d = draw(rng, order, n1, m, lo); nb, bd = d["nb"], d["bd"]
    for r in range(N):
        if r != a: nb[r] = R + ((r + s) % N) * CAPP + rng.integers(0, CAPP, (6, R))
        top = np.where(rng.random(N * CAPP) < 0.5, m[r], n1[r]); e = (rng.random(N * CAPP) * top).astype(np.int64)
        if r == a: e = rng.integers(n1[a], R, N * CAPP)
        if r == b: e = rng.integers(0, m[b], N * CAPP)
        bd[r] = table(order[r][e])
    return d
def setup_inputs_spread(rng):
    d = setup_inputs(rng); d["x"][:, 1:] = wide(rng, N, 16, R)[:, 1:]; return d
def grow(x, nb, bd):
    v = np.concatenate([a.astype(np.float64).T for a in x])
    w = np.stack([entries(a) for a in bd]).astype(np.int64).reshape(N, N, CAPP); near = []
    for r in range(N):
        ext = np.concatenate([r * R + np.arange(R), (R * np.arange(N)[:, None] + w[:, r]).reshape(-1)])
        near.append(ext[nb[r]].T)
    near = np.concatenate(near)
    p = np.flatnonzero(v[:, 0] > T1); number = np.full(N * R, -1); number[p] = np.arange(len(p)); kids = []
    for o in range(8):
        c = v[p].copy()
        for d in range(3): c += 0.125 * (v[near[p, 2 * d + (o >> d & 1)]] - v[p])
        kids.append(c)
    return v, near, p, number, np.stack(kids)
def check_inputs(d):
    bad = []; x = d["x"].astype(np.float32); nb, bd = d["nb"], d["bd"]
    if not np.isfinite(x).all() or not (np.abs(x) <= 65536).all(): bad.append("x finite and of size at most 65536")
    elif (x[:, 0] != np.floor(x[:, 0])).any() or (np.abs(x[:, 0]) > 256).any(): bad.append("x channel 0")
    own = (nb - R) // CAPP == np.arange(N)[:, None, None]
    if (nb < 0).any() or (nb >= R + N * CAPP).any() or own.any(): bad.append("nb")
    if (bd < 0).any() or (bd >= R).any(): bad.append("bd")
    if bad: return bad
    v, near, p, number, c1 = grow(d["x"], nb, bd); q = p // R
    if (np.bincount(q, minlength=N) > S1).any(): bad.append("splits of level 1")
    if (np.bincount(q[np.nonzero(c1[:, :, 0] > T2)[1]], minlength=N) > S2).any(): bad.append("splits of level 2")
    return bad
def reference(x, nb, bd):
    v, near, p, number, c1 = grow(x, nb, bd)
    O, S = np.nonzero(c1[:, :, 0] > T2)
    number2 = np.full(c1.shape[:2], -1); number2[O, S] = np.arange(len(O)); mid = c1[O, S]; val = {}; fine = {}
    for d in range(3):
        for b in range(2):
            m = near[p[S], 2 * d + b]; t = np.where((O >> d & 1) != b, S, number[m]); o = O ^ (1 << d)
            val[d, b] = np.where((t >= 0)[:, None], c1[o, t], v[m]); fine[d, b] = np.where(t >= 0, number2[o, t], -1)
    c2 = []
    for o in range(8):
        c = mid.copy()
        for d in range(3): c += 0.125 * (val[d, o >> d & 1] - mid)
        c2.append(c)
    c2 = np.stack(c2); z = 0.25 * c2
    for o in range(8):
        for d in range(3):
            b = o >> d & 1; other = c2[o ^ (1 << d)]; u = fine[d, b]
            z[o] += 0.125 * (other + np.where((u >= 0)[:, None], other[u], val[d, b]))
    y1 = np.zeros((N, 8, 16, S1)); y2 = np.zeros((N, 8, 16, S2))
    for r in range(N):
        a = c1[:, p // R == r]; y1[r, :, :, :a.shape[1]] = a.transpose(0, 2, 1)
        a = z[:, p[S] // R == r]; y2[r, :, :, :a.shape[1]] = a.transpose(0, 2, 1)
    return {"y1": y1.reshape(N, 128, S1).astype(np.float32), "y2": y2.reshape(N, 128, S2).astype(np.float32)}

from concourse.bass import DstId, RemoteDMATransfer
from concourse.mybir import AluOpType, AxisListType, ActivationFunctionType

R, S1, S2, CAP, NR = 2048, 256, 1024, 16, 8
BIG = 16384.0
XV, XG, XN, XNG, XEND = 256, 2304, 2432, 2688, 2816
U0 = 1024
UC, UI, UV, UT, UEND = U0 + 8, U0 + 392, U0 + 648, U0 + 2696, U0 + 2696 + 8 * 384

F, B, I, U = "float32", "bfloat16", "int32", "uint16"
SHAPES = {
    "XB": (XEND, B), "UW": (UEND, F), "AT": (2432, F), "X0": (16, B), "D1": (256, I), "D1P": (256, F), "WN1": (512, F),
    "BD": (8, I), "BD2": (16, I), "LB": (24, U), "P1": (128, B), "P2": (128, B), "P3": (512, F), "FG": (512, F),
    "IP": (2, I), "PI": (16, I), "PC": (16, F), "PD": (32, F), "IOT": (128, F), "NG": (128, F), "I640": (16, F),
    "E": (128, F), "EH": (128, B), "E0": (128, F), "TM": (64, F), "KT": (288, F), "CD": (168, I), "DI": (168, I), "LM": (168, U),
    "ID": (128, F), "ONES": (128, F), "TRI": (128, B), "CC": (32, F), "DJ": (48, F), "LC": (64, U), "M16": (256, F),
    "M4": (128, F), "RTA": (128, F), "F1": (16, F), "FI1": (16, B),
    "G1": (16, F), "T1": (16, F), "T2": (16, F), "O1": (16, F), "AW": (16, F), "LO": (32, U), "GB1": (128, F), "GB2": (128, F),
    "SC": (256, F), "SD": (256, F), "SE": (128, F), "SF": (128, F), "LN": (32, U), "PL": (16, F), "BA": (48, F), "BB": (48, F),
    "LBB": (40, U), "S8": (256, F), "NS8": (256, F), "AR": (256, F), "ARW": (16, F), "XM": (128, F), "ALR": (128, F), "DEL": (64, F),
    "CS": (64, F), "MC": (128, B), "MI": (128, B), "R0": (64, B), "TH": (128, F), "TF": (1024, F), "TN": (1024, B),
    "FAB": (256, F), "FM": (128, B), "ALF": (128, F), "LT": (64, F), "LT2": (64, F), "LFF": (64, U), "SG": (128, F), "SGH": (128, B),
    "A12": (128, B), "A11": (128, B), "A3": (128, B), "F2": (16, B), "FI2": (16, B), "U1": (16, F), "U2": (16, F), "RT2": (128, F),
    "DA": (256, F), "DB": (256, F), "DH": (256, B), "DV": (256, B), "WN2": (1280, B), "ROLE": (32, F), "BL": (432, B),
    "LG": (192, U), "GA": (1024, F), "GB": (1024, F), "GC": (1024, F), "ZS": (1024, F), "SM": (32, F),
}
SCRATCH = {k: ("sbuf", [128, v[0]], v[1]) for k, v in SHAPES.items()}
for _b in range(8):
    SCRATCH["PS%d" % _b] = ("psum", [128, 512], "float32")
SEMAPHORES = ["ve", "ac", "pe", "po", "lbd", "lx", "lx0", "lnb", "arr1", "arr2", "arr3", "sent", "st"]

op = AluOpType
ADD, SUB, MUL, MAX, MIN = op.add, op.subtract, op.mult, op.max, op.min
EQ, NE, GT, GE, LT, LE = op.is_equal, op.not_equal, op.is_gt, op.is_ge, op.is_lt, op.is_le
SHR, AND = op.logical_shift_right, op.bitwise_and
IDN = ActivationFunctionType.Identity


def bit(x, d):
    return x >> d & 1


def ham(x, y):
    return bin(x ^ y).count("1")


def pair(o):
    return min(o, 7 - o)


def k_face(g, o, e):
    if g == o:
        return 2
    return 1 if ham(g, o) == 1 and not (e ^ o) & (g ^ o) else 0


def k_sib(j, o, e):
    cnt = 3 - ham(e, o)
    if j in (0, 7):
        return cnt if j == 0 else 0
    d, b = (j - 1) // 2, (j - 1) % 2
    same = int(bit(e, d) == bit(o, d))
    return cnt - same if b == bit(o, d) else same


def k_child(j, o):
    if j in (0, 7):
        return int(j == 0)
    return int((j - 1) % 2 == bit(o, (j - 1) // 2))


def k_inward(j, o):
    return k_child(j, o) + (1 if 1 <= j <= 6 else 0)


def served(g, t):
    return t if ham(g, t) <= 1 else 7 - t


def k_role(g, t):
    x = g ^ served(g, t)
    if x == 0:
        return 0
    d = x.bit_length() - 1
    return 2 + 2 * d - bit(g, d)


DROP = ((0, 3), (5, 6))
SMOOTH = (0.0, 0.4375, 0.25, 0.0625, -0.125, 0.125)


def k_smooth(g, n):
    d, e = n // 8, (n % 8) ^ 4
    if g in DROP[d]:
        return SMOOTH.index(0.4375 - 0.1875 * ham(g, e))
    corner = [c for c in DROP[d] if bit(c, d) == bit(g, d)][0]
    w = 0.125 * (e == g ^ (1 << d)) + 0.125 * (3 - 2 * ham(g, corner)) * (e == corner ^ (1 << d))
    return SMOOTH.index(w)


def rank_program(g, core, T, topo):
    rank = T.rank_of(core)
    if rank is None:
        return
    Q = {"ve": g.vector, "ac": g.scalar, "pe": g.tensor, "po": g, "sy": g.sync}
    count = {"ve": 0, "ac": 0, "pe": 0, "po": 0}
    seen = {q: {} for q in Q}
    log = {}

    def a(name, lo=0, hi=None, step=1, p=None):
        if hi is None:
            hi = T[name].shape[1]
        ps = slice(0, 128) if p is None else slice(p[0], p[1])
        ap = T[name][ps, lo:hi] if step == 1 else T[name][ps, lo:hi:step]
        if name.startswith("PS"):
            lo, hi = 0, 512
        return (ap, [(name, lo, hi)])

    def col(name, c):
        return a(name, c, c + 1)

    def ind(win, off):
        return (win[0].indirect(off[0]), win[1] + off[1])

    def wait(q, sem, val):
        if seen[q].get(sem, 0) < val:
            Q[q].wait_ge(T.sem[sem], val)
            seen[q][sem] = val

    def need(q, reads, writes):
        want = {}
        for regs, w in ((reads, False), (writes, True)):
            for name, lo, hi in regs:
                for l, h, pw, pq, sem, val in log.get(name, []):
                    if l < hi and lo < h and (w or pw or (name.startswith("PS") and pq != q)) and not (q == "pe" and pq == "pe"):
                        want[sem] = max(want.get(sem, 0), val)
        for sem in sorted(want):
            wait(q, sem, want[sem])

    def note(q, reads, writes, sem, val):
        for regs, w in ((reads, False), (writes, True)):
            for name, lo, hi in regs:
                log.setdefault(name, []).append((lo, hi, w, q, sem, val))

    def run(q, outs, ins, call):
        reads = [r for x in ins if isinstance(x, tuple) for r in x[1]]
        writes = outs[1][:1]
        reads = reads + outs[1][1:]
        need(q, reads, writes)
        count[q] += 1
        call().then_inc(T.sem[q], 1)
        note(q, reads, writes, q, count[q])

    def v(x):
        return x[0] if isinstance(x, tuple) else x

    def ts(out, x, s1, o0, s2=None, o1=None):
        if o1 is None:
            run("ve", out, [x, s1], lambda: g.vector.tensor_scalar(out[0], x[0], v(s1), None, o0))
        else:
            run("ve", out, [x, s1, s2], lambda: g.vector.tensor_scalar(out[0], x[0], v(s1), v(s2), o0, o1))

    def tt(out, x, y, o):
        run("ve", out, [x, y], lambda: g.vector.tensor_tensor(out[0], x[0], y[0], o))

    def cp(out, x):
        run("ve", out, [x], lambda: g.vector.tensor_copy(out[0], x[0]))

    def ms(out, c):
        run("ve", out, [], lambda: g.vector.memset(out[0], c))

    def scan(out, d0, d1, init, o0, o1):
        run("ve", out, [d0, d1], lambda: g.vector.tensor_tensor_scan(out[0], d0[0], d1[0], init, o0, o1))

    def pick(out, rows, mask):
        scan(out, rows, mask, BIG, MIN, ADD)

    def act(out, x, bias=0.0, scale=1.0):
        run("ac", out, [x, bias, scale], lambda: g.scalar.activation(out[0], x[0], IDN, bias=v(bias), scale=v(scale)))

    def mm(out, w, x, start=True, stop=True):
        run("pe", out, [w, x], lambda: g.tensor.matmul(out[0], w[0], x[0], start, stop))

    def iota(out, pattern, base=0, cm=0):
        if SHAPES[out[1][0][0]][1] == I:
            run("po", out, [], lambda: g.iota(out[0], pattern, base, cm))
        else:
            run("po", out, [], lambda: g.iota(out[0], pattern, base, cm, allow_small_or_imprecise_dtypes=True))

    def select(out, x, pattern, cmp, fill, base, cm):
        run("po", out, [x], lambda: g.affine_select(out[0], x[0], pattern, cmp, fill, base, cm))

    def code2(lo, k):
        c = [sum(k(x, n) << 2 * x for x in range(8)) for n in range(8)]
        iota(a("CD", lo, lo + 8), [[c[4] - c[0], 2], [c[2] - c[0], 2], [c[1] - c[0], 2]], c[0])

    def code3(lo, ks):
        wait("po", "po", count["po"])
        for m in range(0, len(ks), 2):
            for h in range(2):
                c = [sum(ks[m + y](4 * h + x) << 3 * x for x in range(4)) for y in range(2)]
                iota(a("CD", lo + m, lo + m + 2, p=(64 * h, 64 * h + 64)), [[c[1] - c[0], 2]], c[0])
        wait("po", "po", count["po"])

    def decode(lo, hi, c, mask):
        ts(a("DI", lo, hi), a("CD", lo, hi), col("PD", c), MUL, col("PD", c + 1), ADD)
        ts(a("DI", lo, hi), a("DI", lo, hi), mask, AND)

    def exchange(src, width, dst, dst_lo, sem):
        need("po", a(src)[1], [])
        used = []
        transfers = []
        for k in range(1, NR):
            q = (rank + k) % NR
            d = T.cores[q]
            e = [x for x in topo.engines(core, d) if x not in used][0]
            used.append(e)
            rid, pid = topo.addr(d, core)
            transfers.append(RemoteDMATransfer(
                dst_ids=[DstId(rid=rid, pnc=pid)], dma_engine_mask=1 << e, remote_sem=T.sem[sem],
                src=T[src][:, q * width:(q + 1) * width],
                dst=T[dst][:, dst_lo + rank * width:dst_lo + (rank + 1) * width]))
        g.remote_dma_fused(transfers, local_sem=T.sem.sent)

    def landing(name, lo, width, sem):
        for q in range(NR):
            if q != rank:
                note("remote", [], [(name, lo + q * width, lo + (q + 1) * width)], sem, NR - 1)

    landing("XB", XG, CAP, "arr1")
    landing("XB", XNG, CAP, "arr2")
    landing("FG", 0, 4 * CAP, "arr3")

    def pc(c):
        return col("PC", c)

    def pd(c):
        return col("PD", c)

    JJ, GR, G0, RR, J4, JM, J8, PP, DC = 0, 1, 2, 5, 6, 7, 8, 9, 10
    J0, J16, K3, Z0, SN, C1, A4, A8, HF, KK, BETA = 0, 1, 2, 3, 4, 5, 6, 8, 10, 11, 12
    LPERM, LJ, L4, L8, LR0, LF1, LR, LF2 = 0, 16, 32, 40, 48, 52, 56, 60
    CMC, CMI, CF1, CR, CTF, CTN, CSM = 0, 8, 16, 20, 24, 88, 152
    KF, KN, KI, KR, KS = 0, 48, 112, 160, 192
    E16 = a("TM", 32, 48)
    order = [0, 7, 1, 6, 2, 5, 3, 4]

    def faces(n):
        o = order[n]
        cp(a("TF", 128 * o, 128 * o + 128), ind(a("KT", KF, KF + 48), a("LM", CTF + 8 * o, CTF + 8 * o + 8)))

    def own(n):
        o = order[n]
        bank = a("PS%d" % (4 + n % 4), 0, 256)
        mm(bank, a("TN", 128 * o, 128 * o + 128), a("XB", XN, XNG), True, False)
        mm(bank, a("TF", 128 * o, 128 * o + 128), a("UW", 256 * pair(o), 256 * pair(o) + 256), False, True)

    def keep(n):
        act(a("UW", UT + 384 * order[n], UT + 384 * order[n] + 256), a("PS%d" % (4 + n % 4), 0, 256))

    iota(a("IP"), [[1, 2]], 0, 1)
    iota(a("D1"), [[1, 256]], 0, 16)
    iota(a("IOT"), [[1, 128]])
    g.sync.dma_start(T.X0[:, :], T.x[0, :]).then_inc(T.sem.lx0, 16)
    for k in range(8):
        Q["sy" if k < 4 else "ac"].dma_start(T.BD[16 * k:16 * k + 16, :], T.bd[:, :]).then_inc(T.sem.lbd, 16)
    for k in range(8):
        Q["sy" if k < 4 else "ac"].dma_start(T.XB[16 * k:16 * k + 16, XV:XG], T.x[:, :]).then_inc(T.sem.lx, 16)
    need("sy", [], a("D1")[1])
    for k in range(8):
        g.sync.dma_start(T.D1[16 * k + 1:16 * k + 7, :], T.nb[:, 256 * k:256 * k + 256]).then_inc(T.sem.lnb, 16)
    note("dma", [], a("BD")[1], "lbd", 128)
    note("dma", [], a("XB", XV, XG)[1], "lx", 128)
    note("dma", [], a("X0")[1], "lx0", 16)
    note("dma", [], a("D1")[1], "lnb", 128)
    iota(a("I640"), [[1, 16]], 640, 16)
    iota(a("NG"), [[1, 8], [0, 16]])
    code2(CMC, k_child)
    code2(CMI, k_inward)
    code3(CF1, [lambda x, t=t: served(x, t) for t in range(4)] + [lambda x, t=t: k_role(x, t) for t in range(4)])

    ms(a("ONES"), 1.0)
    for c, src, sh, m in ((JJ, 0, 0, 15), (GR, 0, 4, 7), (G0, 0, 4, 1), (G0 + 1, 0, 5, 1), (G0 + 2, 0, 6, 1), (RR, 0, 0, 7),
                          (J4, 0, 2, 3), (JM, 0, 0, 3), (J8, 0, 3, 1), (PP, 0, 0, 127), (DC, 1, 1, 3)):
        ts(col("PI", c), col("IP", src), sh, SHR, m, AND)
    ms(a("XB", 0, XV), 0.0)
    cp(a("PC", 0, 11), a("PI", 0, 11))
    ms(a("XB", XG + CAP * rank, XG + CAP * rank + CAP), 0.0)
    ts(a("LC", LJ, LJ + 16), a("ONES", 0, 16), pc(JJ), MUL)
    ts(pd(J16), pc(JJ), 16.0, MUL)
    ts(pd(J0), pc(JJ), 0.0, EQ)
    ts(E16, a("IOT", 0, 16), pc(JJ), EQ)
    ts(a("TM", 0, 16), a("IOT", 0, 16), pc(JJ), LT, BIG, MUL)
    ts(a("TRI"), a("IOT"), pc(PP), GT)
    ts(a("TM", 48, 64), E16, -BIG, MUL)
    ts(a("CC", 0, 16), a("IOT", 0, 16), 16.0, MUL, pc(JJ), ADD)
    tt(a("TM", 0, 16), a("TM", 0, 16), a("TM", 48, 64), ADD)
    ts(a("F1"), a("X0"), 0.0, GT)
    ts(col("TM", 15), col("TM", 15), 2 * BIG, ADD)
    scan(a("FI1"), a("ONES", 0, 16), a("F1"), 0.0, MUL, ADD)
    mm(a("PS0", 0, 1), a("TRI"), col("FI1", 15))
    ts(a("G1"), a("X0"), 0.0, LE, 4096.0, MUL)
    ts(a("LB", 0, 8), a("BD"), float(XV), ADD)
    tt(a("T1"), a("FI1"), a("G1"), ADD)
    ts(a("DJ", 0, 16), a("CC", 0, 16), 256.0, ADD)
    ts(a("T2"), a("T1"), col("PS0", 0), ADD, -1.0, ADD)
    ts(a("BD2", 0, 8), a("BD"), 15, AND)
    ts(a("BD2", 8, 16), a("BD"), 4, SHR)
    tt(a("AW"), a("T2"), a("I640"), MIN)
    cp(a("LB", 8, 24), a("BD2"))
    tt(a("O1"), a("T2"), a("DJ", 0, 16), MIN)
    ts(a("LC", LPERM, LPERM + 16), a("IOT", 0, 16), pd(J16), ADD)
    cp(a("LO", 0, 16), a("O1"))
    ts(pd(Z0), pc(GR), 0.0, EQ)
    ms(a("WN1", 0, 256), 0.0)
    act(a("AT", 0, 128), a("IOT"), 392.0)
    for n in (128, 256, 512):
        act(a("AT", n, 2 * n), a("AT", 0, n), float(n))
    act(a("AT", 1024, 1536), a("AT", 0, 512), 1024.0)
    act(a("GB1"), ind(a("AW"), a("LB", 8, 16)))

    act(a("P1"), ind(a("XB", 0, XG), a("LB", 0, 8)))
    exchange("P1", CAP, "XB", XG, "arr1")
    for o in range(8):
        code2(CTF + 8 * o, lambda x, e: k_face(x, o, e))
        code2(CTN + 8 * o, lambda x, e: k_sib(x, o, e))
    act(a("M16"), ind(a("TM", 0, 16), a("LC", LJ, LJ + 16)))
    act(a("AT", 1536, 2048), a("AT", 0, 512), 1536.0)
    act(a("E"), ind(E16, a("LC", LJ, LJ + 8)))
    act(a("E0"), a("E"), 0.0, pd(Z0))
    act(a("S8"), a("AT", 0, 256), -384.0)
    act(a("AT", 2048, XG), a("AT", 0, 256), 2048.0)
    act(a("AT", XG, XN), a("IOT"), 264.0)

    ts(a("RTA"), a("NG"), pc(JJ), EQ)
    ts(a("ID"), a("IOT"), pc(PP), EQ)
    ts(a("RTA", 112, 128), a("ONES", 0, 16), pd(J0), MUL)
    ts(a("D1P"), ind(a("D1"), a("LC", LPERM, LPERM + 16)), float(XV), ADD)
    ts(pd(SN), pd(Z0), -4.0 / 64, MUL, -1.0 / 64, ADD)
    cp(ind(a("WN1"), a("LO", 0, 16)), a("D1P"))
    mm(a("PS1", 0, 256), a("RTA"), a("WN1", 0, 256))
    tt(a("GB2"), ind(a("ID"), a("LB", 16, 24)), a("GB1"), MUL)
    mm(a("PS3", 0, 128), a("ONES"), a("GB2"))
    ms(a("KT"), 0.0)
    ts(pd(C1), pd(Z0), 39.0 / 64, MUL, 1.0 / 64, ADD)
    ts(a("TM", 24, 32), a("IOT", 0, 8), pc(GR), NE, 1e9, MUL)
    ts(a("LC", L8, L8 + 8), a("ONES", 0, 8), pc(RR), MUL)
    pick(a("SC"), a("PS1", 0, 256), a("M16"))
    for h in range(2):
        ts(a("KT", KR + 16 + 8 * h, KR + 24 + 8 * h), a("IOT", 0, 8), pc(GR), EQ, pd(J0), MUL)
    ts(a("LN", 0, 16), a("SC", 15, 256, 16), -BIG, ADD)
    mm(a("PS2", 0, 16), a("E0"), a("SC", 15, 256, 16))
    act(a("KT", KN + 16, KN + 32), E16, 0.0, pd(SN))
    act(a("TH"), ind(a("TM", 24, 32), a("LC", L8, L8 + 8)), 100.0)
    act(a("EH"), a("E"))
    act(a("KT", KI + 16, KI + 32), E16, 0.0, pd(C1))
    act(a("KT", KI + 32, KI + 48), E16, 0.0, 7.0 / 64)
    act(a("NS8"), a("S8"), 0.0, -1.0)
    act(a("KT", KF + 16, KF + 32), E16, 0.0, 0.125)
    act(a("KT", KF + 32, KF + 48), E16)
    for k in (2, 3):
        act(a("KT", KN + 16 * k, KN + 16 * k + 16), a("KT", KN + 16, KN + 32), 0.0, float(k))
    act(a("UW", UV, UV + 1024), a("XB", XV, XV + 1024))
    pick(a("SE"), a("PS3", 0, 128), a("M16", 0, 128))
    ts(a("DJ", 16, 32), a("CC", 0, 16), BIG, ADD)
    ts(a("BA", 0, 8), a("SE", 15, 128, 16), BIG + 384.0, LT, 2816.0, MUL)
    ts(a("BB", 0, 8), a("SE", 15, 128, 16), -BIG - 384.0, ADD)
    tt(a("PL"), a("PS2", 0, 16), a("DJ", 16, 32), MAX)
    tt(a("BA", 0, 8), a("BA", 0, 8), a("BB", 0, 8), ADD)
    ts(a("LN", 16, 32), a("PL"), -BIG, ADD)
    cp(a("LBB", 0, 8), a("BA", 0, 8))
    cp(ind(a("AT"), a("LN", 16, 32)), a("S8"))
    for d in range(3):
        ts(col("SM", d), pc(G0 + d), 4.0 ** -(1 << d) - 1, MUL, 1.0, ADD)
    cp(a("AR"), ind(a("AT"), a("LN", 0, 16)))
    ts(pd(A4), col("SM", 0), col("SM", 1), MUL, col("SM", 2), MUL)
    ts(a("SG"), a("NG"), pc(GR), EQ)
    ts(pd(A4 + 1), pd(A4), 0.5, MUL, -0.5, ADD)
    pick(a("SD"), a("AR"), a("M16"))
    decode(CMC, CMI + 8, A4, 3)
    ts(a("ARW"), a("SD", 15, 256, 16), -BIG, ADD)
    ts(a("LM", CMC, CMI + 8), a("DI", CMC, CMI + 8), 16.0, MUL, pc(JJ), ADD)
    tt(a("XM"), ind(a("ARW"), a("LC", LJ, LJ + 8)), a("SG"), MUL)
    mm(a("PS2", 0, 128), a("E"), a("XM"))
    ts(a("SM", 4, 8), a("IOT", 0, 4), 2.0, MUL, pc(J8), ADD)
    ts(a("MC"), ind(a("KT", KN, KN + 32), a("LM", CMC, CMC + 8)), -8.0, MUL)
    ts(a("LC", LR0, LR0 + 4), a("SM", 4, 8), 16.0, MUL)
    ts(col("SM", 0), pc(G0), -7.0 / 8, MUL, 1.0, ADD)
    cp(a("R0"), ind(a("MC"), a("LC", LR0, LR0 + 4)))
    decode(CTF, CSM, A4, 3)
    ts(col("SM", 1), pc(G0 + 1), -63.0 / 64, MUL, 1.0, ADD)
    ts(a("LM", CTF, CSM), a("DI", CTF, CSM), 16.0, MUL, pc(JJ), ADD)

    act(a("XB", XN, XNG), ind(a("XB", 0, XN), a("LN", 0, 16)))
    act(a("P2"), ind(a("XB", 0, XNG), a("LBB", 0, 8)))
    exchange("P2", CAP, "XB", XNG, "arr2")
    iota(a("LT"), [[0, 4], [16, 16]], 8)
    iota(a("A11"), [[0, 128]], 1)
    select(a("A3"), a("A11"), [[16, 8], [0, 16]], GT, 0.0, 0, -1)
    select(a("SGH"), a("A11"), [[-16, 8], [0, 16]], GE, 0.0, 0, 1)
    select(a("SGH"), a("SGH"), [[16, 8], [0, 16]], GE, 0.0, 15, -1)
    iota(a("A11"), [[0, 128]], -1)
    select(a("A11"), a("A11"), [[-1, 128]], GE, 0.0, 0, 1)
    select(a("A11"), a("A11"), [[16, 8], [0, 16]], GE, 0.0, 15, -1)
    select(a("A12"), a("A11"), [[-1, 128]], NE, -2048.0, 0, 1)
    iota(a("WN2", 0, S2), [[0, S2]])

    for h in range(2):
        mm(a("PS0", 64 * h, 64 * h + 64), a("XB", XN + 128 * h, XN + 128 * h + 128), a("R0"))
    mm(a("PS4", 0, 256), a("MC"), a("XB", XN, XNG))
    act(a("ALR"), a("PS2", 0, 128))
    act(a("MI"), ind(a("KT", KI, KI + 48), a("LM", CMI, CMI + 8)))
    mm(a("PS5", 0, 256), a("MI"), a("XB", XN, XNG))
    act(a("LT2"), a("LT"), pc(JJ))
    act(a("UW", UC, UC + 256), a("PS4", 0, 256))
    need("sy", a("UW", UC, UC + 256)[1], [])
    g.sync.dma_start(T.y1[:, :], T.UW[:, UC:UC + 256]).then_inc(T.sem.st, 16)
    act(a("UW", UI, UV), a("PS5", 0, 256))
    act(a("UW", UV + 1024, UT), a("XB", XV + 1024, XG))
    act(a("RT2"), ind(a("KT", KR, KR + 32), a("LM", CMC, CMC + 8)))
    for o in order:
        act(a("TN", 128 * o, 128 * o + 128), ind(a("KT", KN, KN + 64), a("LM", CTN + 8 * o, CTN + 8 * o + 8)))

    tt(pd(A8), col("SM", 0), col("SM", 1), MUL)
    ts(a("TM", 16, 20), a("IOT", 0, 4), pc(J4), LT, BIG, MUL)
    ts(pd(A8 + 1), pd(A8), 0.5, MUL, -0.5, ADD)
    ts(a("TM", 20, 24), a("IOT", 0, 4), pc(J4), EQ, -BIG, MUL)
    ts(a("CC", 16, 32), a("CC", 0, 16), 8.0, ADD)
    decode(CF1, CR + 4, A8, 7)
    ts(pd(HF), pc(J8), 64.0, MUL, pc(RR), ADD)
    ts(a("SM", 12, 16), a("DI", CR, CR + 4), 0.0, EQ, 384.0, MUL)
    ts(a("LC", LR, LR + 4), a("DI", CR, CR + 4), 16.0, MUL, pc(JJ), ADD)
    ts(a("LC", LF1, LF1 + 4), a("DI", CF1, CF1 + 4), 8.0, MUL, pd(HF), ADD)
    for t in range(4):
        ts(a("CS", 16 * t, 16 * t + 16), a("CC", 16, 32), col("SM", 12 + t), SUB)
    tt(a("FM"), a("PS0", 0, 128), a("TH"), GT)
    mm(a("PS1", 0, 128), a("EH"), a("FM"))
    tt(a("TM", 16, 20), a("TM", 16, 20), a("TM", 20, 24), ADD)
    ts(a("LC", L4, L4 + 8), a("ONES", 0, 8), pc(JM), MUL)
    tt(a("DEL"), ind(a("ALR"), a("LC", LR, LR + 4)), a("CS"), SUB)
    ts(col("TM", 19), col("TM", 19), 2 * BIG, ADD)
    cp(a("ALF"), a("PS1", 0, 128))
    ms(a("XB", XNG + CAP * rank, XNG + CAP * rank + CAP), 0.0)
    tt(a("LT"), ind(a("ALF"), a("LC", LF1, LF1 + 4)), a("DEL"), MUL)
    ms(a("UW", U0, UC), 0.0)
    tt(a("LT"), a("LT"), a("LT2"), ADD)
    ts(pd(K3), pc(JM), 256.0, MUL, -1032.0, ADD)
    cp(a("LFF"), a("LT"))
    cp(a("M4"), ind(a("TM", 16, 20), a("LC", L4, L4 + 8)))
    ts(pd(KK), pc(GR), 8.0, MUL, pd(HF), ADD)
    pick(a("SF"), a("PS3", 0, 128), a("M4"))
    ts(a("LC", LF2, LF2 + 1), pd(KK), 0.0, ADD)
    ts(a("BA", 16, 48), a("SF", 3, 128, 4), BIG + 384.0, LT, pd(K3), MUL)
    ts(a("BB", 16, 48), a("SF", 3, 128, 4), 1032.0 - BIG, ADD)
    faces(0)
    tt(a("BA", 16, 48), a("BA", 16, 48), a("BB", 16, 48), ADD)
    faces(1)
    cp(a("LBB", 8, 40), a("BA", 16, 48))
    mm(a("PS2", 0, 256), a("RT2"), a("AR"), True, False)
    mm(a("PS2", 0, 256), a("RT2"), a("NS8"), False, False)
    mm(a("PS2", 0, 256), a("ID"), a("S8"), False, True)
    for d in range(3):
        ts(col("SM", d), pc(G0 + d), -768.0 * (1 << d), MUL, 384.0 * (1 << d), ADD)
    ts(a("SM", 4, 7), a("IOT", 1, 4), pc(DC), EQ)
    ts(pd(KK), pc(GR), 384.0, MUL, 2688.0, ADD)
    tt(a("SM", 0, 3), a("SM", 0, 3), a("SM", 4, 7), MUL)
    ts(pd(BETA), pc(J8), -2.0, MUL, 1.0, ADD)
    run("ve", col("SM", 8), [a("SM", 0, 3)], lambda: g.vector.tensor_reduce(T.SM[:, 8:9], T.SM[:, 0:3], AxisListType.X, ADD))
    ts(a("DJ", 32, 48), a("CC", 0, 16), 1024.0, ADD)
    tt(pd(KK), pd(KK), col("SM", 8), ADD)

    mm(a("PS4", 0, 128), a("MC"), a("XB", XNG, XEND))
    act(a("UW", UC + 256, UI), a("PS4", 0, 128))
    win = a("UW", U0, UT)
    for t in range(4):
        (cp if t % 2 else act)(a("UW", 256 * t, 256 * t + 256), ind(win, a("LFF", 16 * t, 16 * t + 16)))
    for t in range(2):
        (cp if t % 2 else act)(a("P3", 256 * t, 256 * t + 256), ind(a("UW", 0, UT), a("LBB", 8 + 16 * t, 24 + 16 * t)))
    exchange("P3", 4 * CAP, "FG", 0, "arr3")
    iota(a("ROLE", 0, 8), [[0, 4], [-1, 2]], 2)
    iota(a("ROLE", 9, 17), [[0, 2], [-1, 2], [0, 2]], 4)
    iota(a("ROLE", 18, 26), [[-1, 2], [0, 4]], 6)
    iota(a("ROLE", 8, 27, 9), [[0, 3]], -1)
    iota(a("ROLE", 0, 4, 3), [[0, 2]], 0)
    iota(a("ROLE", 14, 16), [[0, 2]], 0)
    iota(a("BL"), [[0, 432]])
    code3(CSM, [lambda x, n=n: k_smooth(x, n) for n in range(16)])

    ts(a("DB"), a("PS2", 0, 256), 392.0, LT, pd(KK), MUL)
    cp(a("F2"), ind(a("ALF"), a("LC", LF2, LF2 + 1)))
    tt(a("DA"), a("PS2", 0, 256), a("DB"), ADD)
    scan(a("FI2"), a("ONES", 0, 16), a("F2"), 0.0, MUL, ADD)
    act(a("DH"), a("DA"))
    act(a("PS1", 0, 256), a("DA"), 0.0, pc(J8))
    act(a("DB"), a("DH"), 0.0, pd(BETA))
    own(0)
    own(1)
    mm(a("PS0", 0, 16), a("A12"), a("F2"), True, False)
    mm(a("PS0", 0, 16), a("SGH"), a("FI2"), False, True)
    mm(a("PS0", 16, 17), a("A3"), col("FI2", 15))
    for n in (2, 3):
        faces(n)
        own(n)
    ts(a("U1"), a("PS0", 0, 16), col("PS0", 16), ADD, 2047.0, ADD)
    keep(0)
    keep(1)
    faces(4)
    tt(a("U2"), a("U1"), a("DJ", 32, 48), MIN)
    faces(5)
    cp(a("LO", 16, 32), a("U2"))
    tt(a("DV"), a("PS1", 0, 256), a("DB"), ADD)
    own(4)
    own(5)
    keep(2)
    keep(3)
    faces(6)
    faces(7)
    own(6)
    own(7)
    cp(ind(a("WN2"), a("LO", 16, 32)), a("DV"))
    ts(a("BL", 15, 432, 16), a("ROLE", 0, 27), pc(RR), EQ)
    for n in range(4, 8):
        keep(n)
    for k in range(3):
        for j in range(16):
            mm(a("PS2", 64 * k, 64 * k + 64), a("BL", 144 * k + 15 - j, 144 * k + 143 - j), a("WN2", j, S2, 16), j == 0, j == 15)
    ms(a("FG", 64 * rank, 64 * rank + 64), 0.0)
    decode(CSM, CSM + 16, A8, 7)
    for k in range(1, 6):
        act(a("KT", KS + 16 * k, KS + 16 * k + 16), E16, 0.0, SMOOTH[k])
    ts(a("LM", CSM, CSM + 16), a("DI", CSM, CSM + 16), 16.0, MUL, pc(JJ), ADD)
    act(a("FAB"), ind(a("KT", KS, KS + 96), a("LM", CSM, CSM + 16)))
    cp(a("LG"), a("PS2", 0, 192))

    banks = [0, 1, 3, 4, 5, 6, 7, 2]
    for o in range(7):
        mm(a("PS%d" % banks[o], 0, 128), a("TN", 128 * o, 128 * o + 128), a("XB", XNG, XEND), True, False)
    for o in range(8):
        bank = a("PS%d" % banks[o], 0, 128)
        if o == 7:
            mm(bank, a("TN", 128 * o, 128 * o + 128), a("XB", XNG, XEND), True, False)
        mm(bank, a("TF", 128 * o, 128 * o + 128), a("FG", pair(o), 512, 4), False, True)
        (cp if o % 2 else act)(a("UW", UT + 384 * o + 256, UT + 384 * o + 384), bank)

    win = a("UW", U0, UEND)
    stores = 1
    edges = (0, 128, 384, 640, 896, 1024)
    for c in range(5):
        lo, hi = edges[c], edges[c + 1]

        def lst(k):
            return ind(win, a("LG", 64 * k + lo // 16, 64 * k + hi // 16))
        act(a("GA", lo, hi), lst(0))
        (act if c else cp)(a("GB", lo, hi), lst(1))
        bank = a("PS%d" % c, 0, hi - lo)
        mm(bank, a("FAB", 0, 128), a("GA", lo, hi), True, False)
        mm(bank, a("FAB", 128, 256), a("GB", lo, hi), False, True)
        ts(a("GC", lo, hi), lst(2), 0.125, MUL)
        tt(a("ZS", lo, hi), bank, a("GC", lo, hi), ADD)
        need("sy", a("ZS", lo, hi)[1], [])
        for h in range(2):
            g.sync.dma_start(T.y2[64 - 64 * h:128 - 64 * h, lo:hi], T.ZS[64 * h:64 * h + 64, lo:hi]).then_inc(T.sem.st, 16)
            stores += 1

    g.wait_ge(T.sem.sent, 3 * (NR - 1))
    wait("po", "po", count["po"])
    for q in ("pe", "ac", "ve"):
        g.sync.wait_ge(T.sem[q], count[q])
    g.sync.wait_ge(T.sem.st, 16 * stores)
